import numpy as np
import ml_dtypes


def mxq(x, axis, fmt="e4m3"):
    dtype, down = {"e4m3": (ml_dtypes.float8_e4m3fn, 7), "e5m2": (ml_dtypes.float8_e5m2, 14)}[fmt]
    v = np.moveaxis(np.asarray(x, np.float32).astype(ml_dtypes.bfloat16).astype(np.float64), axis, -1)
    blocks = v.reshape(v.shape[:-1] + (-1, 32))
    amax = np.abs(blocks).max(-1, keepdims=True)
    byte = np.maximum(np.where(amax > 0, np.frexp(amax)[1] - 1 + 127, 0) - down, 1)
    scale = np.exp2(byte - 127.0)
    codes = (blocks / scale).astype(np.float32).astype(dtype).astype(np.float64)
    return np.moveaxis((codes * scale).reshape(v.shape), -1, axis)


WIDE = False


def mx_kscale(k):
    if not WIDE:
        return np.ones(k)
    levels = np.array([10, -10, 5, -5, 0])
    if k % 512:
        return np.exp2(np.random.permutation(np.resize(levels, k // 32))).repeat(32)
    a = np.empty((k // 512, 16))
    for p in range(k // 512):
        a[p, :8] = np.random.permutation(np.resize(levels, 8))
        for g in range(8):
            far = levels[np.abs(levels - a[p, g]) >= 10]
            a[p, g + 8] = far[np.random.randint(len(far))]
    return np.exp2(a.ravel()).repeat(32)


def f64(x):
    return np.asarray(x).astype(np.float64)


def striped(idx):
    return np.tile(idx.reshape(-1, 16).T, (8, 1)).astype(np.uint16)


def unstriped(offs):
    return offs[:16].T.reshape(-1).astype(np.int64)


def pack_weight(w):
    k, n = w.shape
    w = f64(np.asarray(w, np.float32).astype(ml_dtypes.bfloat16)).reshape(k // 32, 32, n)
    amax = np.abs(w).max(1)
    byte = np.clip(np.where(amax > 0, np.frexp(amax)[1] - 1 + 127 - 7, 1), 1, 254)
    scaled = (w * np.exp2(127.0 - byte)[:, None, :]).reshape(k, n).astype(np.float32)
    words = np.ascontiguousarray(scaled.reshape(k // 512, 128, 4, n).transpose(0, 1, 3, 2)).astype(ml_dtypes.float8_e4m3fn).view(np.uint8)
    return words, np.ascontiguousarray(byte.astype(np.uint8).reshape(k // 512, 16, n))


def unpack_weight(words, scales):
    g, p, n, _ = words.shape
    vals = np.ascontiguousarray(words).view(ml_dtypes.float8_e4m3fn).astype(np.float64) * np.repeat(np.exp2(scales.astype(np.float64) - 127.0), 8, axis=1)[..., None]
    return vals.transpose(0, 1, 3, 2).reshape(g * 512, n)


def relu(v):
    return np.maximum(v, 0.0)


K, T, S, V, N = 1024, 2048, 768, 256, 128
P = 2 ** 7


def setup_inputs():
    n = np.random.standard_normal
    s = mx_kscale(K)[:, None]
    packed_xT = pack_weight(n((K, T)) * s)
    return {
        "x_words": packed_xT[0],
        "x_scales": packed_xT[1],
        "w1": (n((K, N)) / np.sqrt(K) / s).astype(np.float32),
        "margin": np.tile(np.random.uniform(0.2, 2.0, V), (P, 1)).astype(np.float32),
        "offs": striped(np.random.permutation(T)[:S]),
    }


def reference(x_words, x_scales, w1, margin, offs):
    xq = unpack_weight(x_words, x_scales)[:, unstriped(offs)]
    h = mxq(f64(w1), 0, "e4m3").T @ xq
    near = (h[:, :V] - h[:, V:2 * V]) ** 2
    far = (h[:, :V] - h[:, 2 * V:3 * V]) ** 2
    return relu(near - far + f64(margin)[:1])

@@ -1,0 +1,104 @@
+from contextlib import ExitStack
+
+import concourse.mybir as mybir
+
+K, T, S, V, N = 1024, 2048, 768, 256, 128
+FLOPS = 2 * K * S * N
+
+F32 = mybir.dt.float32
+BF16 = mybir.dt.bfloat16
+U32 = mybir.dt.uint32
+I32 = mybir.dt.int32
+U16 = mybir.dt.uint16
+U8 = mybir.dt.uint8
+FP8X4 = mybir.dt.float8_e4m3fn_x4
+ALU = mybir.AluOpType
+ACT = mybir.ActivationFunctionType
+
+P = 128
+PACK = 4
+K_PASS = P * PACK
+LIST_ROWS = 16
+
+
+def tile_picked_triplet_none_p_kernel(tc, x_words, x_scales, w1, margin, offs, out):
+    nc = tc.nc
+    with ExitStack() as ctx:
+        keep = ctx.enter_context(tc.tile_pool(name="keep", bufs=1))
+        psum = ctx.enter_context(tc.psum_pool(name="psum", bufs=1))
+
+        offsets = keep.tile([P, S // LIST_ROWS], U16, name="offsets")
+        table = [keep.tile([P, T], U32, name="table%d" % z, align_bytes=64) for z in range(2)]
+        scale_table = keep.tile([P, T], U8, name="scale_table", align_bytes=64)
+        w_raw = keep.tile([P, 2, PACK, N], F32, name="w_raw")
+        margin_sb = keep.tile([P, V], F32, name="margin_sb")
+
+        def load_words(z):
+            nc.sync.dma_start(table[z][:].bitcast(I32), x_words[z].rearrange("p n t -> p (n t)").bitcast(I32))
+
+        nc.vector.memset(scale_table[:].bitcast(I32), 0)
+        nc.sync.dma_start(offsets[:], offs)
+        nc.sync.dma_start(w_raw[:], w1.rearrange("(z p j) m -> p z j m", p=P, j=PACK))
+        for q in range(4):
+            nc.sync.dma_start(scale_table[32 * q:32 * q + 8, :].bitcast(I32), x_scales[:, 4 * q:4 * q + 4, :].bitcast(I32))
+        load_words(0)
+        load_words(1)
+        nc.sync.dma_start(margin_sb[:], margin)
+
+        w_bf = [keep.tile([P, N, PACK], BF16, name="w_bf%d" % z, align_bytes=64) for z in range(2)]
+        w_codes = [keep.tile([P, N], U32, name="w_codes%d" % z, align_bytes=64) for z in range(2)]
+        w_scales = [keep.tile([P, N], U8, name="w_scales%d" % z, align_bytes=64) for z in range(2)]
+        picked0 = keep.tile([P, S], U32, name="picked0", align_bytes=64)
+        picked1 = [keep.tile([P, V], U32, name="picked1_%d" % i, align_bytes=64) for i in range(3)]
+        picked_scales = keep.tile([P, S], U8, name="picked_scales", align_bytes=64)
+        h = [psum.tile([P, V], F32, name="h%d" % i) for i in range(3)]
+
+        def cast_w(z):
+            nc.scalar.copy(w_bf[z][:], w_raw[:, z].rearrange("p j m -> p m j"))
+
+        def quantize_w(z):
+            nc.vector.quantize_mx(out=w_codes[z][:].bitcast(FP8X4), scales=w_scales[z][:], in_=w_bf[z][:].rearrange("p m j -> p (m j)"))
+
+        def multiply(z, i, words):
+            nc.tensor.matmul_mx(out=h[i][:], lhsT=w_codes[z][:].bitcast(FP8X4), lhsT_scale=w_scales[z][:],
+                                rhs=words.bitcast(FP8X4), rhs_scale=picked_scales[4 * z:P, i * V:(i + 1) * V],
+                                start=(z == 0), stop=(z == 1))
+
+        def gather_third(i):
+            cols = V // LIST_ROWS
+            nc.vector.tensor_copy(picked1[i][:], table[1][:].indirect(offsets[:, i * cols:(i + 1) * cols]))
+
+        cast_w(0)
+        cast_w(1)
+        nc.vector.tensor_copy(picked_scales[:], scale_table[:].indirect(offsets[:]))
+        quantize_w(0)
+        quantize_w(1)
+        nc.vector.tensor_copy(picked0[:], table[0][:].indirect(offsets[:]))
+        for i in range(3):
+            multiply(0, i, picked0[:, i * V:(i + 1) * V])
+        for i in range(3):
+            gather_third(i)
+            multiply(1, i, picked1[i][:])
+
+        anchor = keep.tile([P, V], F32, name="anchor")
+        d_near = keep.tile([P, V], F32, name="d_near")
+        d_far = keep.tile([P, V], F32, name="d_far")
+        near = keep.tile([P, V], F32, name="near")
+        far = keep.tile([P, V], F32, name="far")
+        near_m = keep.tile([P, V], F32, name="near_m")
+        loss = keep.tile([P, V], F32, name="loss")
+        res = keep.tile([P, V], F32, name="res")
+        halves = [slice(0, V // 2), slice(V // 2, V)]
+        nc.scalar.copy(anchor[:], h[0][:])
+        nc.vector.tensor_tensor(d_near[:], anchor[:], h[1][:], ALU.subtract)
+        nc.scalar.activation(near[:], d_near[:], ACT.Square)
+        for c in halves:
+            nc.vector.tensor_tensor(d_far[:, c], anchor[:, c], h[2][:, c], ALU.subtract)
+        for c in halves:
+            nc.scalar.activation(far[:, c], d_far[:, c], ACT.Square)
+        nc.vector.tensor_tensor(near_m[:], near[:], margin_sb[:], ALU.add)
+        for c in halves:
+            nc.vector.tensor_tensor(loss[:, c], near_m[:, c], far[:, c], ALU.subtract)
+        for c in halves:
+            nc.vector.tensor_scalar(res[:, c], loss[:, c], 0.0, None, ALU.max)
+        nc.sync.dma_start(out, res[:])

@@ -29,38 +29,35 @@ def tile_picked_triplet_none_p_kernel(tc, x_words, x_scales, w1, margin, offs, o
 
         offsets = keep.tile([P, S // LIST_ROWS], U16, name="offsets")
         table = [keep.tile([P, T], U32, name="table%d" % z, align_bytes=64) for z in range(2)]
-        scale_table = keep.tile([P, T], U8, name="scale_table", align_bytes=64)
+        scale_table = keep.tile([P, T], U8, name="scale_table", tag="shared", align_bytes=64)
         w_raw = keep.tile([P, 2, PACK, N], F32, name="w_raw")
         margin_sb = keep.tile([P, V], F32, name="margin_sb")
 
         def load_words(z):
             nc.sync.dma_start(table[z][:].bitcast(I32), x_words[z].rearrange("p n t -> p (n t)").bitcast(I32))
 
-        nc.vector.memset(scale_table[:].bitcast(I32), 0)
+        nc.sync.dma_start(scale_table[0:32, :].bitcast(I32), x_scales.rearrange("z q c -> (z q) c").bitcast(I32))
+        nc.vector.memset(scale_table[32:64, :].bitcast(I32), 0)
+        nc.vector.memset(scale_table[64:P, :].bitcast(I32), 0)
         nc.sync.dma_start(offsets[:], offs)
         nc.sync.dma_start(w_raw[:], w1.rearrange("(z p j) m -> p z j m", p=P, j=PACK))
-        for q in range(4):
-            nc.sync.dma_start(scale_table[32 * q:32 * q + 8, :].bitcast(I32), x_scales[:, 4 * q:4 * q + 4, :].bitcast(I32))
         load_words(0)
         load_words(1)
         nc.sync.dma_start(margin_sb[:], margin)
 
-        w_bf = [keep.tile([P, N, PACK], BF16, name="w_bf%d" % z, align_bytes=64) for z in range(2)]
-        w_codes = [keep.tile([P, N], U32, name="w_codes%d" % z, align_bytes=64) for z in range(2)]
-        w_scales = [keep.tile([P, N], U8, name="w_scales%d" % z, align_bytes=64) for z in range(2)]
+        w_bf = keep.tile([P, 2, N, PACK], BF16, name="w_bf", align_bytes=64)
+        w_scales = keep.tile([P, 2, N], U8, name="w_scales", align_bytes=64)
         picked0 = keep.tile([P, S], U32, name="picked0", align_bytes=64)
         picked1 = [keep.tile([P, V], U32, name="picked1_%d" % i, align_bytes=64) for i in range(3)]
+        picked_rows = keep.tile([P, S], U8, name="picked_rows", align_bytes=64)
         picked_scales = keep.tile([P, S], U8, name="picked_scales", align_bytes=64)
         h = [psum.tile([P, V], F32, name="h%d" % i) for i in range(3)]
 
         def cast_w(z):
-            nc.scalar.copy(w_bf[z][:], w_raw[:, z].rearrange("p j m -> p m j"))
-
-        def quantize_w(z):
-            nc.vector.quantize_mx(out=w_codes[z][:].bitcast(FP8X4), scales=w_scales[z][:], in_=w_bf[z][:].rearrange("p m j -> p (m j)"))
+            nc.scalar.copy(w_bf[:, z], w_raw[:, z].rearrange("p j m -> p m j"))
 
         def multiply(z, i, words):
-            nc.tensor.matmul_mx(out=h[i][:], lhsT=w_codes[z][:].bitcast(FP8X4), lhsT_scale=w_scales[z][:],
+            nc.tensor.matmul_mx(out=h[i][:], lhsT=w_codes[:, z].bitcast(FP8X4), lhsT_scale=w_scales[:, z],
                                 rhs=words.bitcast(FP8X4), rhs_scale=picked_scales[4 * z:P, i * V:(i + 1) * V],
                                 start=(z == 0), stop=(z == 1))
 
@@ -70,9 +67,16 @@ def tile_picked_triplet_none_p_kernel(tc, x_words, x_scales, w1, margin, offs, o
 
         cast_w(0)
         cast_w(1)
-        nc.vector.tensor_copy(picked_scales[:], scale_table[:].indirect(offsets[:]))
-        quantize_w(0)
-        quantize_w(1)
+        nc.vector.tensor_copy(picked_rows[:], scale_table[:].indirect(offsets[:]))
+        nc.vector.tensor_copy(picked_scales[:].bitcast(I32), picked_rows[:].bitcast(I32))
+        for z in range(2):
+            for q in range(4):
+                src, dst = 16 * z + 4 * q, 32 * q + 4 * z
+                if src != dst:
+                    nc.scalar.dma_start(picked_scales[dst:dst + 4, :].bitcast(I32), picked_rows[src:src + 4, :].bitcast(I32))
+        w_codes = keep.tile([P, 2, N], U32, name="w_codes", tag="shared", align_bytes=64)
+        nc.vector.quantize_mx(out=w_codes[:].rearrange("p z m -> p (z m)").bitcast(FP8X4), scales=w_scales[:].rearrange("p z m -> p (z m)"),
+                              in_=w_bf[:].rearrange("p z m j -> p (z m j)"))
         nc.vector.tensor_copy(picked0[:], table[0][:].indirect(offsets[:]))
         for i in range(3):
             multiply(0, i, picked0[:, i * V:(i + 1) * V])
@@ -90,15 +94,19 @@ def tile_picked_triplet_none_p_kernel(tc, x_words, x_scales, w1, margin, offs, o
         res = keep.tile([P, V], F32, name="res")
         halves = [slice(0, V // 2), slice(V // 2, V)]
         nc.scalar.copy(anchor[:], h[0][:])
-        nc.vector.tensor_tensor(d_near[:], anchor[:], h[1][:], ALU.subtract)
-        nc.scalar.activation(near[:], d_near[:], ACT.Square)
+        for c in halves:
+            nc.vector.tensor_tensor(d_near[:, c], anchor[:, c], h[1][:, c], ALU.subtract)
+        for c in halves:
+            nc.scalar.activation(near[:, c], d_near[:, c], ACT.Square)
         for c in halves:
             nc.vector.tensor_tensor(d_far[:, c], anchor[:, c], h[2][:, c], ALU.subtract)
         for c in halves:
             nc.scalar.activation(far[:, c], d_far[:, c], ACT.Square)
-        nc.vector.tensor_tensor(near_m[:], near[:], margin_sb[:], ALU.add)
+        for c in halves:
+            nc.vector.tensor_tensor(near_m[:, c], near[:, c], margin_sb[:, c], ALU.add)
         for c in halves:
             nc.vector.tensor_tensor(loss[:, c], near_m[:, c], far[:, c], ALU.subtract)
         for c in halves:
             nc.vector.tensor_scalar(res[:, c], loss[:, c], 0.0, None, ALU.max)
-        nc.sync.dma_start(out, res[:])
+        for c, queue in zip(halves, (nc.scalar, nc.sync)):
+            queue.dma_start(out[:, c], res[:, c])

@@ -28,10 +28,9 @@ def tile_picked_triplet_none_p_kernel(tc, x_words, x_scales, w1, margin, offs, o
         psum = ctx.enter_context(tc.psum_pool(name="psum", bufs=1))
 
         offsets = keep.tile([P, S // LIST_ROWS], U16, name="offsets")
-        table = [keep.tile([P, T], U32, name="table%d" % z, align_bytes=64) for z in range(2)]
+        table = [keep.tile([P, T], U32, name="table%d" % z, tag="table%d" % z, align_bytes=64) for z in range(2)]
         scale_table = keep.tile([P, T], U8, name="scale_table", tag="shared", align_bytes=64)
         w_raw = keep.tile([P, 2, PACK, N], F32, name="w_raw")
-        margin_sb = keep.tile([P, V], F32, name="margin_sb")
 
         def load_words(z):
             nc.sync.dma_start(table[z][:].bitcast(I32), x_words[z].rearrange("p n t -> p (n t)").bitcast(I32))
@@ -43,7 +42,6 @@ def tile_picked_triplet_none_p_kernel(tc, x_words, x_scales, w1, margin, offs, o
         nc.sync.dma_start(w_raw[:], w1.rearrange("(z p j) m -> p z j m", p=P, j=PACK))
         load_words(0)
         load_words(1)
-        nc.sync.dma_start(margin_sb[:], margin)
 
         w_bf = keep.tile([P, 2, N, PACK], BF16, name="w_bf", align_bytes=64)
         w_scales = keep.tile([P, 2, N], U8, name="w_scales", align_bytes=64)
@@ -73,15 +71,16 @@ def tile_picked_triplet_none_p_kernel(tc, x_words, x_scales, w1, margin, offs, o
             for q in range(4):
                 src, dst = 16 * z + 4 * q, 32 * q + 4 * z
                 if src != dst:
-                    nc.scalar.dma_start(picked_scales[dst:dst + 4, :].bitcast(I32), picked_rows[src:src + 4, :].bitcast(I32))
+                    nc.sync.dma_start(picked_scales[dst:dst + 4, :].bitcast(I32), picked_rows[src:src + 4, :].bitcast(I32))
         w_codes = keep.tile([P, 2, N], U32, name="w_codes", tag="shared", align_bytes=64)
         nc.vector.quantize_mx(out=w_codes[:].rearrange("p z m -> p (z m)").bitcast(FP8X4), scales=w_scales[:].rearrange("p z m -> p (z m)"),
                               in_=w_bf[:].rearrange("p z m j -> p (z m j)"))
         nc.vector.tensor_copy(picked0[:], table[0][:].indirect(offsets[:]))
-        for i in range(3):
-            multiply(0, i, picked0[:, i * V:(i + 1) * V])
+        margin_sb = keep.tile([P, V], F32, name="margin_sb", tag="table0", align_bytes=64)
+        nc.sync.dma_start(margin_sb[:], margin)
         for i in range(3):
             gather_third(i)
+            multiply(0, i, picked0[:, i * V:(i + 1) * V])
             multiply(1, i, picked1[i][:])
 
         anchor = keep.tile([P, V], F32, name="anchor")

@@ -35,7 +35,7 @@ def tile_picked_triplet_none_p_kernel(tc, x_words, x_scales, w1, margin, offs, o
         def load_words(z):
             nc.sync.dma_start(table[z][:].bitcast(I32), x_words[z].rearrange("p n t -> p (n t)").bitcast(I32))
 
-        nc.sync.dma_start(scale_table[0:32, :].bitcast(I32), x_scales.rearrange("z q c -> (z q) c").bitcast(I32))
+        nc.scalar.dma_start(scale_table[0:32, :].bitcast(I32), x_scales.rearrange("z q c -> (z q) c").bitcast(I32))
         nc.vector.memset(scale_table[32:64, :].bitcast(I32), 0)
         nc.vector.memset(scale_table[64:P, :].bitcast(I32), 0)
         nc.sync.dma_start(offsets[:], offs)
@@ -48,15 +48,21 @@ def tile_picked_triplet_none_p_kernel(tc, x_words, x_scales, w1, margin, offs, o
         picked0 = keep.tile([P, S], U32, name="picked0", align_bytes=64)
         picked1 = [keep.tile([P, V], U32, name="picked1_%d" % i, align_bytes=64) for i in range(3)]
         picked_rows = keep.tile([P, S], U8, name="picked_rows", align_bytes=64)
-        picked_scales = keep.tile([P, S], U8, name="picked_scales", align_bytes=64)
-        h = [psum.tile([P, V], F32, name="h%d" % i) for i in range(3)]
+        picked_scales = [keep.tile([P, S], U8, name="picked_scales%d" % z, align_bytes=64) for z in range(2)]
+        nc.vector.memset(picked_scales[0][32:64, :].bitcast(I32), 0)
+        nc.vector.memset(picked_scales[0][64:P, :].bitcast(I32), 0)
+        nc.vector.memset(picked_scales[1][:].bitcast(I32), 0)
+        halves = [slice(0, V // 2), slice(V // 2, V)]
+        h = [psum.tile([P, V], F32, name="h%d" % i) for i in range(2)]
+        h_far = [psum.tile([P, V // 2], F32, name="h_far%d" % i) for i in range(2)]
 
         def cast_w(z):
             nc.scalar.copy(w_bf[:, z], w_raw[:, z].rearrange("p j m -> p m j"))
 
-        def multiply(z, i, words):
-            nc.tensor.matmul_mx(out=h[i][:], lhsT=w_codes[:, z].bitcast(FP8X4), lhsT_scale=w_scales[:, z],
-                                rhs=words.bitcast(FP8X4), rhs_scale=picked_scales[4 * z:P, i * V:(i + 1) * V],
+        def multiply(z, i, acc, cols):
+            words = picked0[:, i * V + cols.start:i * V + cols.stop] if z == 0 else picked1[i][:, cols]
+            nc.tensor.matmul_mx(out=acc[:], lhsT=w_codes[:, z].bitcast(FP8X4), lhsT_scale=w_scales[:, z],
+                                rhs=words.bitcast(FP8X4), rhs_scale=picked_scales[z][:, i * V + cols.start:i * V + cols.stop],
                                 start=(z == 0), stop=(z == 1))
 
         def gather_third(i):
@@ -66,12 +72,12 @@ def tile_picked_triplet_none_p_kernel(tc, x_words, x_scales, w1, margin, offs, o
         cast_w(0)
         cast_w(1)
         nc.vector.tensor_copy(picked_rows[:], scale_table[:].indirect(offsets[:]))
-        nc.vector.tensor_copy(picked_scales[:].bitcast(I32), picked_rows[:].bitcast(I32))
+        nc.vector.tensor_copy(picked_scales[0][0:32, :].bitcast(I32), picked_rows[0:32, :].bitcast(I32))
         for z in range(2):
             for q in range(4):
-                src, dst = 16 * z + 4 * q, 32 * q + 4 * z
+                src, dst = 16 * z + 4 * q, 32 * q
                 if src != dst:
-                    nc.sync.dma_start(picked_scales[dst:dst + 4, :].bitcast(I32), picked_rows[src:src + 4, :].bitcast(I32))
+                    nc.sync.dma_start(picked_scales[z][dst:dst + 4, :].bitcast(I32), picked_rows[src:src + 4, :].bitcast(I32))
         w_codes = keep.tile([P, 2, N], U32, name="w_codes", tag="shared", align_bytes=64)
         nc.vector.quantize_mx(out=w_codes[:].rearrange("p z m -> p (z m)").bitcast(FP8X4), scales=w_scales[:].rearrange("p z m -> p (z m)"),
                               in_=w_bf[:].rearrange("p z m j -> p (z m j)"))
@@ -80,8 +86,12 @@ def tile_picked_triplet_none_p_kernel(tc, x_words, x_scales, w1, margin, offs, o
         nc.sync.dma_start(margin_sb[:], margin)
         for i in range(3):
             gather_third(i)
-            multiply(0, i, picked0[:, i * V:(i + 1) * V])
-            multiply(1, i, picked1[i][:])
+        for z in range(2):
+            for i in range(2):
+                multiply(z, i, h[i], slice(0, V))
+        for z in range(2):
+            for acc, c in zip(h_far, halves):
+                multiply(z, 2, acc, c)
 
         anchor = keep.tile([P, V], F32, name="anchor")
         d_near = keep.tile([P, V], F32, name="d_near")
@@ -91,14 +101,13 @@ def tile_picked_triplet_none_p_kernel(tc, x_words, x_scales, w1, margin, offs, o
         near_m = keep.tile([P, V], F32, name="near_m")
         loss = keep.tile([P, V], F32, name="loss")
         res = keep.tile([P, V], F32, name="res")
-        halves = [slice(0, V // 2), slice(V // 2, V)]
         nc.scalar.copy(anchor[:], h[0][:])
         for c in halves:
             nc.vector.tensor_tensor(d_near[:, c], anchor[:, c], h[1][:, c], ALU.subtract)
         for c in halves:
             nc.scalar.activation(near[:, c], d_near[:, c], ACT.Square)
-        for c in halves:
-            nc.vector.tensor_tensor(d_far[:, c], anchor[:, c], h[2][:, c], ALU.subtract)
+        for acc, c in zip(h_far, halves):
+            nc.vector.tensor_tensor(d_far[:, c], anchor[:, c], acc[:], ALU.subtract)
         for c in halves:
             nc.scalar.activation(far[:, c], d_far[:, c], ACT.Square)
         for c in halves:

@@ -25,12 +25,13 @@ def tile_picked_triplet_none_p_kernel(tc, x_words, x_scales, w1, margin, offs, o
     nc = tc.nc
     with ExitStack() as ctx:
         keep = ctx.enter_context(tc.tile_pool(name="keep", bufs=1))
+        reuse = ctx.enter_context(tc.tile_pool(name="reuse", bufs=1))
         psum = ctx.enter_context(tc.psum_pool(name="psum", bufs=1))
 
         offsets = keep.tile([P, S // LIST_ROWS], U16, name="offsets")
         table = [keep.tile([P, T], U32, name="table%d" % z, tag="table%d" % z, align_bytes=64) for z in range(2)]
         scale_table = keep.tile([P, T], U8, name="scale_table", tag="shared", align_bytes=64)
-        w_raw = keep.tile([P, 2, PACK, N], F32, name="w_raw")
+        w_raw = reuse.tile([P, 2, PACK, N], F32, name="w_raw", tag="raw", align_bytes=64)
 
         def load_words(z):
             nc.sync.dma_start(table[z][:].bitcast(I32), x_words[z].rearrange("p n t -> p (n t)").bitcast(I32))
@@ -43,26 +44,23 @@ def tile_picked_triplet_none_p_kernel(tc, x_words, x_scales, w1, margin, offs, o
         load_words(0)
         load_words(1)
 
-        w_bf = keep.tile([P, 2, N, PACK], BF16, name="w_bf", align_bytes=64)
+        w_bf = [keep.tile([P, N, PACK], BF16, name="w_bf%d" % z, align_bytes=64) for z in range(2)]
         w_scales = keep.tile([P, 2, N], U8, name="w_scales", align_bytes=64)
-        picked0 = keep.tile([P, S], U32, name="picked0", align_bytes=64)
         picked1 = [keep.tile([P, V], U32, name="picked1_%d" % i, align_bytes=64) for i in range(3)]
         picked_rows = keep.tile([P, S], U8, name="picked_rows", align_bytes=64)
-        picked_scales = [keep.tile([P, S], U8, name="picked_scales%d" % z, align_bytes=64) for z in range(2)]
-        nc.vector.memset(picked_scales[0][32:64, :].bitcast(I32), 0)
-        nc.vector.memset(picked_scales[0][64:P, :].bitcast(I32), 0)
-        nc.vector.memset(picked_scales[1][:].bitcast(I32), 0)
+        planes = keep.tile([P, S + 2 * V], U8, name="planes", align_bytes=64)
+        nc.vector.memset(planes[:].bitcast(I32), 0)
         halves = [slice(0, V // 2), slice(V // 2, V)]
         h = [psum.tile([P, V], F32, name="h%d" % i) for i in range(2)]
         h_far = [psum.tile([P, V // 2], F32, name="h_far%d" % i) for i in range(2)]
 
         def cast_w(z):
-            nc.scalar.copy(w_bf[:, z], w_raw[:, z].rearrange("p j m -> p m j"))
+            nc.scalar.copy(w_bf[z][:].rearrange("p (c i) j -> p c j i", i=4), w_raw[:, z].rearrange("p j (c i) -> p c j i", i=4))
 
         def multiply(z, i, acc, cols):
             words = picked0[:, i * V + cols.start:i * V + cols.stop] if z == 0 else picked1[i][:, cols]
             nc.tensor.matmul_mx(out=acc[:], lhsT=w_codes[:, z].bitcast(FP8X4), lhsT_scale=w_scales[:, z],
-                                rhs=words.bitcast(FP8X4), rhs_scale=picked_scales[z][:, i * V + cols.start:i * V + cols.stop],
+                                rhs=words.bitcast(FP8X4), rhs_scale=planes[4 * z:P, (2 * z + i) * V + cols.start:(2 * z + i) * V + cols.stop],
                                 start=(z == 0), stop=(z == 1))
 
         def gather_third(i):
@@ -72,26 +70,29 @@ def tile_picked_triplet_none_p_kernel(tc, x_words, x_scales, w1, margin, offs, o
         cast_w(0)
         cast_w(1)
         nc.vector.tensor_copy(picked_rows[:], scale_table[:].indirect(offsets[:]))
-        nc.vector.tensor_copy(picked_scales[0][0:32, :].bitcast(I32), picked_rows[0:32, :].bitcast(I32))
+        nc.vector.tensor_copy(planes[0:4, 0:S].bitcast(I32), picked_rows[0:4, :].bitcast(I32))
         for z in range(2):
             for q in range(4):
-                src, dst = 16 * z + 4 * q, 32 * q
+                src, dst = 16 * z + 4 * q, 32 * q + 4 * z
                 if src != dst:
-                    nc.sync.dma_start(picked_scales[z][dst:dst + 4, :].bitcast(I32), picked_rows[src:src + 4, :].bitcast(I32))
+                    nc.sync.dma_start(planes[dst:dst + 4, 2 * V * z:2 * V * z + S].bitcast(I32), picked_rows[src:src + 4, :].bitcast(I32))
         w_codes = keep.tile([P, 2, N], U32, name="w_codes", tag="shared", align_bytes=64)
-        nc.vector.quantize_mx(out=w_codes[:].rearrange("p z m -> p (z m)").bitcast(FP8X4), scales=w_scales[:].rearrange("p z m -> p (z m)"),
-                              in_=w_bf[:].rearrange("p z m j -> p (z m j)"))
+        for z in range(2):
+            nc.vector.quantize_mx(out=w_codes[:, z].bitcast(FP8X4), scales=w_scales[:, z], in_=w_bf[z][:].rearrange("p m j -> p (m j)"))
+        picked0 = reuse.tile([P, S], U32, name="picked0", tag="raw", align_bytes=64)
         nc.vector.tensor_copy(picked0[:], table[0][:].indirect(offsets[:]))
         margin_sb = keep.tile([P, V], F32, name="margin_sb", tag="table0", align_bytes=64)
         nc.sync.dma_start(margin_sb[:], margin)
         for i in range(3):
             gather_third(i)
-        for z in range(2):
-            for i in range(2):
-                multiply(z, i, h[i], slice(0, V))
-        for z in range(2):
-            for acc, c in zip(h_far, halves):
-                multiply(z, 2, acc, c)
+        multiply(0, 0, h[0], slice(0, V))
+        multiply(0, 1, h[1], slice(0, V))
+        multiply(1, 0, h[0], slice(0, V))
+        for acc, c in zip(h_far, halves):
+            multiply(0, 2, acc, c)
+        multiply(1, 1, h[1], slice(0, V))
+        for acc, c in zip(h_far, halves):
+            multiply(1, 2, acc, c)
 
         anchor = keep.tile([P, V], F32, name="anchor")
         d_near = keep.tile([P, V], F32, name="d_near")

@@ -51,7 +51,8 @@ def tile_picked_triplet_none_p_kernel(tc, x_words, x_scales, w1, margin, offs, o
         planes = keep.tile([P, S + 2 * V], U8, name="planes", align_bytes=64)
         nc.vector.memset(planes[:].bitcast(I32), 0)
         halves = [slice(0, V // 2), slice(V // 2, V)]
-        h = [psum.tile([P, V], F32, name="h%d" % i) for i in range(2)]
+        h_anchor = psum.tile([P, V], F32, name="h_anchor")
+        h_near = [psum.tile([P, V // 2], F32, name="h_near%d" % i) for i in range(2)]
         h_far = [psum.tile([P, V // 2], F32, name="h_far%d" % i) for i in range(2)]
 
         def cast_w(z):
@@ -85,12 +86,14 @@ def tile_picked_triplet_none_p_kernel(tc, x_words, x_scales, w1, margin, offs, o
         nc.sync.dma_start(margin_sb[:], margin)
         for i in range(3):
             gather_third(i)
-        multiply(0, 0, h[0], slice(0, V))
-        multiply(0, 1, h[1], slice(0, V))
-        multiply(1, 0, h[0], slice(0, V))
-        for acc, c in zip(h_far, halves):
-            multiply(0, 2, acc, c)
-        multiply(1, 1, h[1], slice(0, V))
+        multiply(0, 0, h_anchor, slice(0, V))
+        for acc, c in zip(h_near, halves):
+            multiply(0, 1, acc, c)
+        multiply(1, 0, h_anchor, slice(0, V))
+        multiply(0, 2, h_far[0], halves[0])
+        for acc, c in zip(h_near, halves):
+            multiply(1, 1, acc, c)
+        multiply(0, 2, h_far[1], halves[1])
         for acc, c in zip(h_far, halves):
             multiply(1, 2, acc, c)
 
@@ -102,9 +105,9 @@ def tile_picked_triplet_none_p_kernel(tc, x_words, x_scales, w1, margin, offs, o
         near_m = keep.tile([P, V], F32, name="near_m")
         loss = keep.tile([P, V], F32, name="loss")
         res = keep.tile([P, V], F32, name="res")
-        nc.scalar.copy(anchor[:], h[0][:])
-        for c in halves:
-            nc.vector.tensor_tensor(d_near[:, c], anchor[:, c], h[1][:, c], ALU.subtract)
+        nc.scalar.copy(anchor[:], h_anchor[:])
+        for acc, c in zip(h_near, halves):
+            nc.vector.tensor_tensor(d_near[:, c], anchor[:, c], acc[:], ALU.subtract)
         for c in halves:
             nc.scalar.activation(near[:, c], d_near[:, c], ACT.Square)
         for acc, c in zip(h_far, halves):

@@ -19,6 +19,7 @@ P = 128
 PACK = 4
 K_PASS = P * PACK
 LIST_ROWS = 16
+SHIFT = V + V // 2
 
 
 def tile_picked_triplet_none_p_kernel(tc, x_words, x_scales, w1, margin, offs, out):
@@ -46,9 +47,10 @@ def tile_picked_triplet_none_p_kernel(tc, x_words, x_scales, w1, margin, offs, o
 
         w_bf = [keep.tile([P, N, PACK], BF16, name="w_bf%d" % z, align_bytes=64) for z in range(2)]
         w_scales = keep.tile([P, 2, N], U8, name="w_scales", align_bytes=64)
-        picked1 = [keep.tile([P, V], U32, name="picked1_%d" % i, align_bytes=64) for i in range(3)]
+        picked1 = [keep.tile([P, V], U32, name="picked1_%d" % i, align_bytes=64) for i in range(2)]
+        picked1_far = [keep.tile([P, V // 2], U32, name="picked1_far%d" % i, align_bytes=64) for i in range(2)]
         picked_rows = keep.tile([P, S], U8, name="picked_rows", align_bytes=64)
-        planes = keep.tile([P, S + 2 * V], U8, name="planes", align_bytes=64)
+        planes = keep.tile([P, S + SHIFT], U8, name="planes", align_bytes=64)
         nc.vector.memset(planes[:].bitcast(I32), 0)
         halves = [slice(0, V // 2), slice(V // 2, V)]
         h_anchor = psum.tile([P, V], F32, name="h_anchor")
@@ -59,9 +61,14 @@ def tile_picked_triplet_none_p_kernel(tc, x_words, x_scales, w1, margin, offs, o
             nc.scalar.copy(w_bf[z][:].rearrange("p (c i) j -> p c j i", i=4), w_raw[:, z].rearrange("p j (c i) -> p c j i", i=4))
 
         def multiply(z, i, acc, cols):
-            words = picked0[:, i * V + cols.start:i * V + cols.stop] if z == 0 else picked1[i][:, cols]
+            if z == 0:
+                words = picked0[:, i * V + cols.start:i * V + cols.stop]
+            elif i < 2:
+                words = picked1[i][:, cols]
+            else:
+                words = picked1_far[cols.start // (V // 2)][:]
             nc.tensor.matmul_mx(out=acc[:], lhsT=w_codes[:, z].bitcast(FP8X4), lhsT_scale=w_scales[:, z],
-                                rhs=words.bitcast(FP8X4), rhs_scale=planes[4 * z:P, (2 * z + i) * V + cols.start:(2 * z + i) * V + cols.stop],
+                                rhs=words.bitcast(FP8X4), rhs_scale=planes[4 * z:P, SHIFT * z + i * V + cols.start:SHIFT * z + i * V + cols.stop],
                                 start=(z == 0), stop=(z == 1))
 
         def gather_third(i):
@@ -76,7 +83,7 @@ def tile_picked_triplet_none_p_kernel(tc, x_words, x_scales, w1, margin, offs, o
             for q in range(4):
                 src, dst = 16 * z + 4 * q, 32 * q + 4 * z
                 if src != dst:
-                    nc.sync.dma_start(planes[dst:dst + 4, 2 * V * z:2 * V * z + S].bitcast(I32), picked_rows[src:src + 4, :].bitcast(I32))
+                    nc.sync.dma_start(planes[dst:dst + 4, SHIFT * z:SHIFT * z + S].bitcast(I32), picked_rows[src:src + 4, :].bitcast(I32))
         w_codes = keep.tile([P, 2, N], U32, name="w_codes", tag="shared", align_bytes=64)
         for z in range(2):
             nc.vector.quantize_mx(out=w_codes[:, z].bitcast(FP8X4), scales=w_scales[:, z], in_=w_bf[z][:].rearrange("p m j -> p (m j)"))
@@ -84,18 +91,20 @@ def tile_picked_triplet_none_p_kernel(tc, x_words, x_scales, w1, margin, offs, o
         nc.vector.tensor_copy(picked0[:], table[0][:].indirect(offsets[:]))
         margin_sb = keep.tile([P, V], F32, name="margin_sb", tag="table0", align_bytes=64)
         nc.sync.dma_start(margin_sb[:], margin)
-        for i in range(3):
+        for i in range(2):
             gather_third(i)
+        for dst, c in zip(picked1_far, halves):
+            nc.vector.tensor_copy(dst[:], table[1][:].indirect(offsets[:, (2 * V + c.start) // LIST_ROWS:(2 * V + c.stop) // LIST_ROWS]))
         multiply(0, 0, h_anchor, slice(0, V))
-        for acc, c in zip(h_near, halves):
-            multiply(0, 1, acc, c)
+        multiply(0, 1, h_near[0], halves[0])
         multiply(1, 0, h_anchor, slice(0, V))
-        multiply(0, 2, h_far[0], halves[0])
+        multiply(0, 1, h_near[1], halves[1])
         for acc, c in zip(h_near, halves):
             multiply(1, 1, acc, c)
+        multiply(0, 2, h_far[0], halves[0])
+        multiply(1, 2, h_far[0], halves[0])
         multiply(0, 2, h_far[1], halves[1])
-        for acc, c in zip(h_far, halves):
-            multiply(1, 2, acc, c)
+        multiply(1, 2, h_far[1], halves[1])
 
         anchor = keep.tile([P, V], F32, name="anchor")
         d_near = keep.tile([P, V], F32, name="d_near")

@@ -40,8 +40,8 @@ def tile_picked_triplet_none_p_kernel(tc, x_words, x_scales, w1, margin, offs, o
         nc.scalar.dma_start(scale_table[0:32, :].bitcast(I32), x_scales.rearrange("z q c -> (z q) c").bitcast(I32))
         nc.vector.memset(scale_table[32:64, :].bitcast(I32), 0)
         nc.vector.memset(scale_table[64:P, :].bitcast(I32), 0)
-        nc.sync.dma_start(offsets[:], offs)
         nc.sync.dma_start(w_raw[:], w1.rearrange("(z p j) m -> p z j m", p=P, j=PACK))
+        nc.sync.dma_start(offsets[:], offs)
         load_words(0)
         load_words(1)
 

@@ -30,7 +30,7 @@ def tile_picked_triplet_none_p_kernel(tc, x_words, x_scales, w1, margin, offs, o
         psum = ctx.enter_context(tc.psum_pool(name="psum", bufs=1))
 
         offsets = keep.tile([P, S // LIST_ROWS], U16, name="offsets")
-        table = [keep.tile([P, T], U32, name="table%d" % z, tag="table%d" % z, align_bytes=64) for z in range(2)]
+        table = [keep.tile([P, T], U32, name="table%d" % z, align_bytes=64) for z in range(2)]
         scale_table = keep.tile([P, T], U8, name="scale_table", tag="shared", align_bytes=64)
         w_raw = reuse.tile([P, 2, PACK, N], F32, name="w_raw", tag="raw", align_bytes=64)
 
@@ -49,7 +49,7 @@ def tile_picked_triplet_none_p_kernel(tc, x_words, x_scales, w1, margin, offs, o
         w_scales = keep.tile([P, 2, N], U8, name="w_scales", align_bytes=64)
         picked1 = [keep.tile([P, V], U32, name="picked1_%d" % i, align_bytes=64) for i in range(2)]
         picked1_far = [keep.tile([P, V // 2], U32, name="picked1_far%d" % i, align_bytes=64) for i in range(2)]
-        picked_rows = keep.tile([P, S], U8, name="picked_rows", align_bytes=64)
+        picked_rows = keep.tile([P, S], U8, name="picked_rows", tag="rows", align_bytes=64)
         planes = keep.tile([P, S + SHIFT], U8, name="planes", align_bytes=64)
         nc.vector.memset(planes[:].bitcast(I32), 0)
         halves = [slice(0, V // 2), slice(V // 2, V)]
@@ -89,7 +89,7 @@ def tile_picked_triplet_none_p_kernel(tc, x_words, x_scales, w1, margin, offs, o
             nc.vector.quantize_mx(out=w_codes[:, z].bitcast(FP8X4), scales=w_scales[:, z], in_=w_bf[z][:].rearrange("p m j -> p (m j)"))
         picked0 = reuse.tile([P, S], U32, name="picked0", tag="raw", align_bytes=64)
         nc.vector.tensor_copy(picked0[:], table[0][:].indirect(offsets[:]))
-        margin_sb = keep.tile([P, V], F32, name="margin_sb", tag="table0", align_bytes=64)
+        margin_sb = keep.tile([P, V], F32, name="margin_sb", tag="rows", align_bytes=64)
         nc.sync.dma_start(margin_sb[:], margin)
         for i in range(2):
             gather_third(i)

@@ -51,7 +51,6 @@ def tile_picked_triplet_none_p_kernel(tc, x_words, x_scales, w1, margin, offs, o
         picked1_far = [keep.tile([P, V // 2], U32, name="picked1_far%d" % i, align_bytes=64) for i in range(2)]
         picked_rows = keep.tile([P, S], U8, name="picked_rows", tag="rows", align_bytes=64)
         planes = keep.tile([P, S + SHIFT], U8, name="planes", align_bytes=64)
-        nc.vector.memset(planes[:].bitcast(I32), 0)
         halves = [slice(0, V // 2), slice(V // 2, V)]
         h_anchor = psum.tile([P, V], F32, name="h_anchor")
         h_near = [psum.tile([P, V // 2], F32, name="h_near%d" % i) for i in range(2)]

from contextlib import ExitStack

import concourse.mybir as mybir

K, T, S, V, N = 1024, 2048, 768, 256, 128
FLOPS = 2 * K * S * N

F32 = mybir.dt.float32
BF16 = mybir.dt.bfloat16
U32 = mybir.dt.uint32
I32 = mybir.dt.int32
U16 = mybir.dt.uint16
U8 = mybir.dt.uint8
FP8X4 = mybir.dt.float8_e4m3fn_x4
ALU = mybir.AluOpType
ACT = mybir.ActivationFunctionType

P = 128
PACK = 4
K_PASS = P * PACK
LIST_ROWS = 16
SHIFT = V + V // 2


def tile_picked_triplet_none_p_kernel(tc, x_words, x_scales, w1, margin, offs, out):
    nc = tc.nc
    with ExitStack() as ctx:
        keep = ctx.enter_context(tc.tile_pool(name="keep", bufs=1))
        reuse = ctx.enter_context(tc.tile_pool(name="reuse", bufs=1))
        psum = ctx.enter_context(tc.psum_pool(name="psum", bufs=1))

        offsets = keep.tile([P, S // LIST_ROWS], U16, name="offsets")
        table = [keep.tile([P, T], U32, name="table%d" % z, align_bytes=64) for z in range(2)]
        scale_table = keep.tile([P, T], U8, name="scale_table", tag="shared", align_bytes=64)
        w_raw = reuse.tile([P, 2, PACK, N], F32, name="w_raw", tag="raw", align_bytes=64)

        def load_words(z):
            nc.sync.dma_start(table[z][:].bitcast(I32), x_words[z].rearrange("p n t -> p (n t)").bitcast(I32))

        nc.scalar.dma_start(scale_table[0:32, :].bitcast(I32), x_scales.rearrange("z q c -> (z q) c").bitcast(I32))
        nc.vector.memset(scale_table[32:64, :].bitcast(I32), 0)
        nc.vector.memset(scale_table[64:P, :].bitcast(I32), 0)
        nc.sync.dma_start(w_raw[:], w1.rearrange("(z p j) m -> p z j m", p=P, j=PACK))
        nc.sync.dma_start(offsets[:], offs)
        load_words(0)
        load_words(1)

        w_bf = [keep.tile([P, N, PACK], BF16, name="w_bf%d" % z, align_bytes=64) for z in range(2)]
        w_scales = keep.tile([P, 2, N], U8, name="w_scales", align_bytes=64)
        picked1 = [keep.tile([P, V], U32, name="picked1_%d" % i, align_bytes=64) for i in range(2)]
        picked1_far = [keep.tile([P, V // 2], U32, name="picked1_far%d" % i, align_bytes=64) for i in range(2)]
        picked_rows = keep.tile([P, S], U8, name="picked_rows", tag="rows", align_bytes=64)
        planes = keep.tile([P, S + SHIFT], U8, name="planes", align_bytes=64)
        halves = [slice(0, V // 2), slice(V // 2, V)]
        h_anchor = psum.tile([P, V], F32, name="h_anchor")
        h_near = [psum.tile([P, V // 2], F32, name="h_near%d" % i) for i in range(2)]
        h_far = [psum.tile([P, V // 2], F32, name="h_far%d" % i) for i in range(2)]

        def cast_w(z):
            nc.scalar.copy(w_bf[z][:].rearrange("p (c i) j -> p c j i", i=4), w_raw[:, z].rearrange("p j (c i) -> p c j i", i=4))

        def multiply(z, i, acc, cols):
            if z == 0:
                words = picked0[:, i * V + cols.start:i * V + cols.stop]
            elif i < 2:
                words = picked1[i][:, cols]
            else:
                words = picked1_far[cols.start // (V // 2)][:]
            nc.tensor.matmul_mx(out=acc[:], lhsT=w_codes[:, z].bitcast(FP8X4), lhsT_scale=w_scales[:, z],
                                rhs=words.bitcast(FP8X4), rhs_scale=planes[4 * z:P, SHIFT * z + i * V + cols.start:SHIFT * z + i * V + cols.stop],
                                start=(z == 0), stop=(z == 1))

        def gather_third(i):
            cols = V // LIST_ROWS
            nc.vector.tensor_copy(picked1[i][:], table[1][:].indirect(offsets[:, i * cols:(i + 1) * cols]))

        cast_w(0)
        cast_w(1)
        nc.vector.tensor_copy(picked_rows[:], scale_table[:].indirect(offsets[:]))
        nc.vector.tensor_copy(planes[0:4, 0:S].bitcast(I32), picked_rows[0:4, :].bitcast(I32))
        for z in range(2):
            for q in range(4):
                src, dst = 16 * z + 4 * q, 32 * q + 4 * z
                if src != dst:
                    nc.sync.dma_start(planes[dst:dst + 4, SHIFT * z:SHIFT * z + S].bitcast(I32), picked_rows[src:src + 4, :].bitcast(I32))
        w_codes = keep.tile([P, 2, N], U32, name="w_codes", tag="shared", align_bytes=64)
        for z in range(2):
            nc.vector.quantize_mx(out=w_codes[:, z].bitcast(FP8X4), scales=w_scales[:, z], in_=w_bf[z][:].rearrange("p m j -> p (m j)"))
        picked0 = reuse.tile([P, S], U32, name="picked0", tag="raw", align_bytes=64)
        nc.vector.tensor_copy(picked0[:], table[0][:].indirect(offsets[:]))
        margin_sb = keep.tile([P, V], F32, name="margin_sb", tag="rows", align_bytes=64)
        nc.sync.dma_start(margin_sb[:], margin)
        for i in range(2):
            gather_third(i)
        for dst, c in zip(picked1_far, halves):
            nc.vector.tensor_copy(dst[:], table[1][:].indirect(offsets[:, (2 * V + c.start) // LIST_ROWS:(2 * V + c.stop) // LIST_ROWS]))
        multiply(0, 0, h_anchor, slice(0, V))
        multiply(0, 1, h_near[0], halves[0])
        multiply(1, 0, h_anchor, slice(0, V))
        multiply(0, 1, h_near[1], halves[1])
        for acc, c in zip(h_near, halves):
            multiply(1, 1, acc, c)
        multiply(0, 2, h_far[0], halves[0])
        multiply(1, 2, h_far[0], halves[0])
        multiply(0, 2, h_far[1], halves[1])
        multiply(1, 2, h_far[1], halves[1])

        anchor = keep.tile([P, V], F32, name="anchor")
        d_near = keep.tile([P, V], F32, name="d_near")
        d_far = keep.tile([P, V], F32, name="d_far")
        near = keep.tile([P, V], F32, name="near")
        far = keep.tile([P, V], F32, name="far")
        near_m = keep.tile([P, V], F32, name="near_m")
        loss = keep.tile([P, V], F32, name="loss")
        res = keep.tile([P, V], F32, name="res")
        nc.scalar.copy(anchor[:], h_anchor[:])
        for acc, c in zip(h_near, halves):
            nc.vector.tensor_tensor(d_near[:, c], anchor[:, c], acc[:], ALU.subtract)
        for c in halves:
            nc.scalar.activation(near[:, c], d_near[:, c], ACT.Square)
        for acc, c in zip(h_far, halves):
            nc.vector.tensor_tensor(d_far[:, c], anchor[:, c], acc[:], ALU.subtract)
        for c in halves:
            nc.scalar.activation(far[:, c], d_far[:, c], ACT.Square)
        for c in halves:
            nc.vector.tensor_tensor(near_m[:, c], near[:, c], margin_sb[:, c], ALU.add)
        for c in halves:
            nc.vector.tensor_tensor(loss[:, c], near_m[:, c], far[:, c], ALU.subtract)
        for c in halves:
            nc.vector.tensor_scalar(res[:, c], loss[:, c], 0.0, None, ALU.max)
        for c, queue in zip(halves, (nc.scalar, nc.sync)):
            queue.dma_start(out[:, c], res[:, c])
